import numpy as np
import ml_dtypes


def mxq(x, axis, fmt="e4m3"):
    dtype, down = {"e4m3": (ml_dtypes.float8_e4m3fn, 7), "e5m2": (ml_dtypes.float8_e5m2, 14)}[fmt]
    v = np.moveaxis(np.asarray(x, np.float32).astype(ml_dtypes.bfloat16).astype(np.float64), axis, -1)
    blocks = v.reshape(v.shape[:-1] + (-1, 32))
    amax = np.abs(blocks).max(-1, keepdims=True)
    byte = np.maximum(np.where(amax > 0, np.frexp(amax)[1] - 1 + 127, 0) - down, 1)
    scale = np.exp2(byte - 127.0)
    codes = (blocks / scale).astype(np.float32).astype(dtype).astype(np.float64)
    return np.moveaxis((codes * scale).reshape(v.shape), -1, axis)


WIDE = False


def mx_kscale(k):
    if not WIDE:
        return np.ones(k)
    levels = np.array([10, -10, 5, -5, 0])
    if k % 512:
        return np.exp2(np.random.permutation(np.resize(levels, k // 32))).repeat(32)
    a = np.empty((k // 512, 16))
    for p in range(k // 512):
        a[p, :8] = np.random.permutation(np.resize(levels, 8))
        for g in range(8):
            far = levels[np.abs(levels - a[p, g]) >= 10]
            a[p, g + 8] = far[np.random.randint(len(far))]
    return np.exp2(a.ravel()).repeat(32)


def f64(x):
    return np.asarray(x).astype(np.float64)


def striped(idx):
    return np.tile(idx.reshape(-1, 16).T, (8, 1)).astype(np.uint16)


def unstriped(offs):
    return offs[:16].T.reshape(-1).astype(np.int64)


E2M1 = np.array([0.0, 0.5, 1.0, 1.5, 2.0, 3.0, 4.0, 6.0, -0.0, -0.5, -1.0, -1.5, -2.0, -3.0, -4.0, -6.0])


def pack_weight(w, fmt):
    k, n = w.shape
    w = f64(np.asarray(w, np.float32).astype(ml_dtypes.bfloat16)).reshape(k // 32, 32, n)
    amax = np.abs(w).max(1)
    if fmt == "e4m3":
        byte = np.frexp(amax)[1] - 1 + 127 - 7
    else:
        mant, ex = np.frexp(amax / 6.0)
        byte = np.where(mant > 0.5, ex, ex - 1) + 127
    byte = np.clip(np.where(amax > 0, byte, 1), 1, 254)
    scaled = (w * np.exp2(127.0 - byte)[:, None, :]).reshape(k, n).astype(np.float32)
    by_word = np.ascontiguousarray(scaled.reshape(k // 512, 128, 4, n).transpose(0, 1, 3, 2))
    if fmt == "e4m3":
        words = by_word.astype(ml_dtypes.float8_e4m3fn).view(np.uint8)
    else:
        c = by_word.astype(ml_dtypes.float4_e2m1fn).view(np.uint8) & 0xF
        words = (c[..., 0::2] | (c[..., 1::2] << 4)).reshape(k // 512, 128, 2 * n)
    return np.ascontiguousarray(words), np.ascontiguousarray(byte.astype(np.uint8).reshape(k // 512, 16, n))


def unpack_weight(words, scales, fmt):
    g, _, n = scales.shape
    words = np.ascontiguousarray(words).reshape(g, 128, n, -1)
    if fmt == "e4m3":
        vals = words.view(ml_dtypes.float8_e4m3fn).astype(np.float64)
    else:
        nib = np.empty((g, 128, n, 4), np.uint8)
        nib[..., 0::2] = words & 0xF
        nib[..., 1::2] = words >> 4
        vals = E2M1[nib]
    vals = vals * np.repeat(np.exp2(scales.astype(np.float64) - 127.0), 8, axis=1)[..., None]
    return vals.transpose(0, 1, 3, 2).reshape(g * 512, n)


def gelu(v):
    return 0.5 * v * (1.0 + np.tanh(np.sqrt(2.0 / np.pi) * (v + 0.044715 * v**3)))


K, T, E, C, H, N = 1024, 768, 6, 256, 512, 128


def by_expert(wq, xq):
    return np.concatenate([wq[e].T @ xq[:, e * C:(e + 1) * C] for e in range(E)], axis=1)


def setup_inputs():
    n = np.random.standard_normal
    s = mx_kscale(K)[:, None]
    u = mx_kscale(H)
    first = np.random.permutation(np.repeat(np.arange(E), T // E))
    second = (first + 1 + np.random.permutation(np.repeat(np.arange(E - 1), -(-T // (E - 1)))[:T])) % E
    while np.bincount(second, minlength=E).max() != T // E:
        load = np.bincount(second, minlength=E); hi, lo = int(load.argmax()), int(load.argmin())
        t = np.flatnonzero((second == hi) & (first != lo))[0]; second[t] = lo
    slot_token = np.empty(E * C, np.int64); pos = np.empty((2, T), np.int64); fill = np.zeros(E, np.int64)
    place = np.stack([np.random.permutation(C) for _ in range(E)])
    for r, deal in enumerate((first, second)):
        for t in np.random.permutation(T):
            e = deal[t]; j = e * C + place[e, fill[e]]; fill[e] += 1; slot_token[j] = t; pos[r, t] = j
    g = np.random.uniform(0.2, 0.8, T)
    w1 = [pack_weight(m, "e2m1") for m in n((E + 1, K, H)) / np.sqrt(K) / s[None] * u[None, None, :]]
    w2 = [pack_weight(m, "e2m1") for m in n((E + 1, H, N)) / np.sqrt(H) / u[None, :, None]]
    x = pack_weight(n((K, T)) * s, "e4m3")
    return {
        "x_words": x[0],
        "x_scales": x[1],
        "w1_words": np.stack([m[0] for m in w1]),
        "w1_scales": np.stack([m[1] for m in w1]),
        "w2_words": np.stack([m[0] for m in w2]),
        "w2_scales": np.stack([m[1] for m in w2]),
        "gate": np.stack([np.tile(g, (N, 1)), np.tile(1.0 - g, (N, 1))]).astype(np.float32),
        "offs": striped(slot_token),
        "pos1": striped(pos[0]),
        "pos2": striped(pos[1]),
    }


def reference(x_words, x_scales, w1_words, w1_scales, w2_words, w2_scales, gate, offs, pos1, pos2):
    idx = unstriped(offs)
    w1 = np.stack([unpack_weight(w1_words[e], w1_scales[e], "e2m1") for e in range(E + 1)])
    w2 = np.stack([unpack_weight(w2_words[e], w2_scales[e], "e2m1") for e in range(E + 1)])
    w1q, w2q = w1, w2
    xs = unpack_weight(x_words, x_scales, "e4m3")
    hs = gelu(w1q[E].T @ xs)
    ys = w2q[E].T @ mxq(hs, 0, "e4m3")
    xq = unpack_weight(x_words, x_scales, "e4m3")[:, idx]
    h = gelu(by_expert(w1q, xq))
    y = by_expert(w2q, mxq(h, 0, "e4m3"))
    return ys + f64(gate[0]) * y[:, unstriped(pos1)] + f64(gate[1]) * y[:, unstriped(pos2)]

@@ -1,0 +1,192 @@
+from contextlib import ExitStack
+
+import concourse.mybir as mybir
+from concourse.masks import make_identity
+
+K, T, E, C, H, N = 1024, 768, 6, 256, 512, 128
+FLOPS = 2 * (E * C + T) * (K * H + H * N)
+
+F32 = mybir.dt.float32
+BF16 = mybir.dt.bfloat16
+I32 = mybir.dt.int32
+U32 = mybir.dt.uint32
+U16 = mybir.dt.uint16
+U8 = mybir.dt.uint8
+FP8X4 = mybir.dt.float8_e4m3fn_x4
+FP4X4 = mybir.dt.float4_e2m1fn_x4
+GELU = mybir.ActivationFunctionType.Gelu_apprx_tanh
+MULT = mybir.AluOpType.mult
+ADD = mybir.AluOpType.add
+
+P = 128
+S = E * C
+PAIR = 2 * C
+ORDER = (4, 5, 2, 3, 0, 1)
+
+
+def tile_moe_shr_mlp_gelu_kernel(tc, x_words, x_scales, w1_words, w1_scales, w2_words, w2_scales, gate, offs, pos1, pos2, out):
+    nc = tc.nc
+    with ExitStack() as ctx:
+        keep = ctx.enter_context(tc.tile_pool(name="keep", bufs=1))
+        ring = ctx.enter_context(tc.tile_pool(name="ring", bufs=4))
+        psum = ctx.enter_context(tc.psum_pool(name="psum", bufs=1))
+
+        offs_sb = keep.tile([P, S // 16], U16, name="offs_sb")
+        pos_sb = [keep.tile([P, T // 16], U16, name=f"pos{r}_sb") for r in range(2)]
+        xw = [keep.tile([P, T], I32, name=f"xw{o}", align_bytes=64) for o in range(2)]
+        xs = keep.tile([P, 2, T], U8, name="xs", align_bytes=64)
+        w1s_hi = keep.tile([P, 6, H], U8, name="w1s_hi", align_bytes=64)
+        w1s_lo = keep.tile([P, 8, H], U8, name="w1s_lo", align_bytes=64)
+        w2s = keep.tile([P, E + 1, N], U8, name="w2s", align_bytes=64)
+        ident = keep.tile([P, P], F32, name="ident")
+        warm_in = keep.tile([P, 1], F32, name="warm_in", tag="w_shared", align_bytes=64)
+        warm_out = keep.tile([P, 1], F32, name="warm_out", tag="w_mid", align_bytes=64)
+        y_sb = keep.tile([P, S], F32, name="y_sb")
+        planes = keep.tile([P, 9, C], U8, name="planes", align_bytes=64)
+        acc = [psum.tile([P, H], F32, name=f"acc{b}") for b in range(3)]
+        spare = [psum.tile([P, H], F32, name=f"spare{b}") for b in range(5)]
+
+        def flat(t):
+            return t[:].rearrange("p a b -> p (a b)").bitcast(I32)
+
+        nc.vector.memset(flat(xs), 0)
+        nc.gpsimd.memset(warm_in[:], 0.0)
+        nc.scalar.activation(warm_out[:], warm_in[:], GELU)
+        nc.vector.memset(flat(w1s_hi), 0)
+        make_identity(nc, ident[:])
+        nc.gpsimd.memset(flat(w1s_lo), 0)
+        nc.gpsimd.memset(flat(w2s), 0)
+
+        w1_all = w1_words.rearrange("e s p b -> p (e s) b").bitcast(I32)
+        w1w = {}
+
+        def load_w1(t, at, e0, count):
+            nc.sync.dma_start(t[:, 2 * at : 2 * (at + count), :].bitcast(I32), w1_all[:, 2 * e0 : 2 * (e0 + count), :])
+            for i in range(count):
+                w1w[e0 + i] = [t[:, 2 * (at + i) + o, :] for o in range(2)]
+
+        def load_planes(eng, dst, src):
+            for q in range(4):
+                eng.dma_start(dst[32 * q : 32 * q + 4].bitcast(I32), src[:, 4 * q : 4 * q + 4, :].rearrange("a r n -> r a n").bitcast(I32))
+
+        gw, gs = {}, {}
+
+        def gather(e):
+            slots = offs_sb[:, 16 * e : 16 * (e + 1)]
+            for o in range(2):
+                gs[e, o] = ring.tile([P, C], U8, name=f"gs{o}", align_bytes=64, bufs=2)
+                nc.vector.tensor_copy(gs[e, o][:], xs[:, o, :].indirect(slots))
+            for o in range(2):
+                gw[e, o] = ring.tile([P, C], U32, name=f"gw{o}", align_bytes=64, bufs=2)
+                nc.vector.tensor_copy(gw[e, o][:], xw[o][:].bitcast(U32).indirect(slots))
+
+        w1s_all = w1_scales.rearrange("e s q n -> (e s) q n")
+        w_shared = keep.tile([P, 2, 2 * H], U8, name="w_shared", tag="w_shared", align_bytes=64)
+        w_mid = keep.tile([P, 8, 2 * H], U8, name="w_mid", tag="w_mid", align_bytes=64)
+        nc.sync.dma_start(offs_sb[:], offs)
+        load_planes(nc.sync, xs, x_scales)
+        nc.sync.dma_start(pos_sb[0][:], pos1)
+        nc.sync.dma_start(pos_sb[1][:], pos2)
+        for o in range(2):
+            nc.sync.dma_start(xw[o][:], x_words[o].rearrange("p t r -> p (t r)").bitcast(I32))
+        load_planes(nc.sync, w1s_hi, w1s_all[8:14])
+        load_w1(w_shared, 0, 6, 1)
+        load_w1(w_mid, 2, 4, 2)
+        load_planes(nc.sync, w1s_lo, w1s_all[0:8])
+        load_w1(w_mid, 0, 2, 2)
+        load_planes(nc.sync, w2s, w2_scales.rearrange("e s q n -> (e s) q n"))
+
+        def w1_plane(e, o):
+            return w1s_hi[:, 2 * (e - 4) + o, :] if e >= 4 else w1s_lo[:, 2 * e + o, :]
+
+        def routed_operands(e, j, o):
+            return gw[e, o][:, j * P : (j + 1) * P], gs[e, o][:, j * P : (j + 1) * P]
+
+        def shared_operands(g, j, o):
+            cols = slice(g * C + j * P, g * C + (j + 1) * P)
+            return xw[o][:, cols], xs[:, o, cols]
+
+        def hidden(step, e, operands, bank, copy_out, tags=None, cols_tag=None):
+            tb = bank[:].rearrange("p (j u s) -> p j u s", j=2, u=2)
+            halves = []
+            for j in range(2):
+                a = acc[(2 * step + j) % 3]
+                for o in range(2):
+                    words, scales = operands(j, o)
+                    nc.tensor.matmul_mx(a[:], lhsT=words.bitcast(FP8X4), lhsT_scale=scales, rhs=w1w[e][o].bitcast(FP4X4), rhs_scale=w1_plane(e, o), start=(o == 0), stop=(o == 1))
+                if tags:
+                    h_rows = keep.tile([P, H], BF16, name="h_first", tag=tags[j], align_bytes=64)
+                else:
+                    h_rows = ring.tile([P, H], BF16, name="h_rows")
+                nc.scalar.activation(h_rows[:].rearrange("p (u m d) -> p u m d", u=2, d=2), a[:].rearrange("p (m u d) -> p u m d", u=2, d=2), GELU)
+                halves.append(h_rows)
+            for j in range(2):
+                for u in range(2):
+                    nc.tensor.transpose(tb[:, j, u, :], halves[j][:].bitcast(F32)[:, u * P : (u + 1) * P], ident[:])
+            if cols_tag:
+                h_cols = keep.tile([P, 4 * C], BF16, name="h_late", tag=cols_tag, align_bytes=64)
+            else:
+                h_cols = ring.tile([P, 4 * C], BF16, name="h_cols", align_bytes=64, bufs=7)
+            copy_out(h_cols[:].bitcast(F32).rearrange("p (j s u) -> p j s u", j=2, u=2), tb.rearrange("p j u s -> p j s u"))
+            return h_cols
+
+        on_scalar, on_vector = nc.scalar.copy, nc.vector.tensor_copy
+        h = {}
+        gather(ORDER[0])
+        gather(ORDER[1])
+        h[6] = hidden(0, E, lambda j, o: shared_operands(0, j, o), spare[0], on_scalar, ("w_last", "w2"))
+        w_last = keep.tile([P, 4, 2 * H], U8, name="w_last", tag="w_last", align_bytes=64)
+        load_w1(w_last, 0, 0, 2)
+        w2w = keep.tile([P, E + 1, 2 * N], U8, name="w2w", tag="w2", align_bytes=64)
+        nc.sync.dma_start(w2w[:].bitcast(I32), w2_words.rearrange("e s p b -> p (e s) b").bitcast(I32))
+        turn = {4: spare[1], 5: spare[0], 2: spare[1], 3: spare[2], 0: spare[3], 1: spare[0]}
+        for n, e in enumerate(ORDER):
+            h[e] = hidden(n + 1, e, lambda j, o: routed_operands(e, j, o), turn[e], on_scalar if n < 4 else on_vector, ("gate", "gate2") if n == 0 else None)
+            if n + 2 < E:
+                gather(ORDER[n + 2])
+            if n == 0:
+                gate_sb = keep.tile([P, 2, T], F32, name="gate_sb", tag="gate", align_bytes=64)
+                nc.sync.dma_start(gate_sb[:], gate.rearrange("r n t -> n r t"))
+
+        codes = keep.tile([P, 9, C], U32, name="codes", tag="w_mid", align_bytes=64)
+
+        def quantise(u):
+            nc.vector.quantize_mx(out=codes[:, u, :].bitcast(FP8X4), scales=planes[:, u, :], in_=h[u][:])
+
+        def second(u, dst):
+            e = min(u, E)
+            nc.tensor.matmul_mx(dst, lhsT=w2w[:, e, :].bitcast(FP4X4), lhsT_scale=w2s[:, e, :], rhs=codes[:, u, :].bitcast(FP8X4), rhs_scale=planes[:, u, :], start=True, stop=True)
+
+        for c, bank in ((2, spare[2]), (1, spare[3])):
+            for e in (2 * c, 2 * c + 1):
+                quantise(e)
+                second(e, bank[:, (e % 2) * C : (e % 2 + 1) * C])
+            nc.scalar.copy(y_sb[:, c * PAIR : (c + 1) * PAIR], bank[:])
+        for e in (0, 1):
+            quantise(e)
+            bank = (spare[4], spare[1])[e]
+            second(e, bank[:, 0:C])
+            (on_scalar, on_vector)[e](y_sb[:, e * C : (e + 1) * C], bank[:, 0:C])
+        ys = [spare[2][:, 0:C], spare[3][:, 0:C], spare[4][:, 0:C]]
+        quantise(6)
+        second(6, ys[0])
+        for g in (1, 2):
+            h[6 + g] = hidden(6 + g, E, lambda j, o: shared_operands(g, j, o), spare[g - 1], on_scalar, None, f"late{g}")
+            quantise(6 + g)
+            second(6 + g, ys[g])
+
+        for g in range(3):
+            tok = slice(g * C, (g + 1) * C)
+            parts = []
+            for r in range(2):
+                if r == 0:
+                    part = keep.tile([P, C], F32, name="part0", tag=f"late{g}", align_bytes=64)
+                else:
+                    part = keep.tile([P, C], F32, name="part1")
+                nc.vector.tensor_tensor(part[:], y_sb[:].indirect(pos_sb[r][:, 16 * g : 16 * (g + 1)]), gate_sb[:, r, tok], MULT)
+                parts.append(part)
+            partial = ring.tile([P, C], F32, name="partial")
+            nc.vector.tensor_tensor(partial[:], parts[0][:], ys[g], ADD)
+            total = ring.tile([P, C], F32, name="total")
+            nc.vector.tensor_tensor(total[:], partial[:], parts[1][:], ADD)
+            nc.sync.dma_start(out[:, tok], total[:])

@@ -21,7 +21,7 @@ ADD = mybir.AluOpType.add
 P = 128
 S = E * C
 PAIR = 2 * C
-ORDER = (4, 5, 2, 3, 0, 1)
+ORDER = (5, 4, 3, 2, 1, 0)
 
 
 def tile_moe_shr_mlp_gelu_kernel(tc, x_words, x_scales, w1_words, w1_scales, w2_words, w2_scales, gate, offs, pos1, pos2, out):
@@ -37,14 +37,12 @@ def tile_moe_shr_mlp_gelu_kernel(tc, x_words, x_scales, w1_words, w1_scales, w2_
         xs = keep.tile([P, 2, T], U8, name="xs", align_bytes=64)
         w1s_hi = keep.tile([P, 6, H], U8, name="w1s_hi", align_bytes=64)
         w1s_lo = keep.tile([P, 8, H], U8, name="w1s_lo", align_bytes=64)
-        w2s = keep.tile([P, E + 1, N], U8, name="w2s", align_bytes=64)
         ident = keep.tile([P, P], F32, name="ident")
-        warm_in = keep.tile([P, 1], F32, name="warm_in", tag="w_shared", align_bytes=64)
-        warm_out = keep.tile([P, 1], F32, name="warm_out", tag="w_mid", align_bytes=64)
+        warm_in = keep.tile([P, 1], F32, name="warm_in", tag="w6", align_bytes=64)
+        warm_out = keep.tile([P, 1], F32, name="warm_out", tag="w2345", align_bytes=64)
         y_sb = keep.tile([P, S], F32, name="y_sb")
         planes = keep.tile([P, 9, C], U8, name="planes", align_bytes=64)
-        acc = [psum.tile([P, H], F32, name=f"acc{b}") for b in range(3)]
-        spare = [psum.tile([P, H], F32, name=f"spare{b}") for b in range(5)]
+        banks = [psum.tile([P, H], F32, name=f"bank{b}") for b in range(8)]
 
         def flat(t):
             return t[:].rearrange("p a b -> p (a b)").bitcast(I32)
@@ -55,46 +53,43 @@ def tile_moe_shr_mlp_gelu_kernel(tc, x_words, x_scales, w1_words, w1_scales, w2_
         nc.vector.memset(flat(w1s_hi), 0)
         make_identity(nc, ident[:])
         nc.gpsimd.memset(flat(w1s_lo), 0)
-        nc.gpsimd.memset(flat(w2s), 0)
 
         w1_all = w1_words.rearrange("e s p b -> p (e s) b").bitcast(I32)
         w1w = {}
 
-        def load_w1(t, at, e0, count):
-            nc.sync.dma_start(t[:, 2 * at : 2 * (at + count), :].bitcast(I32), w1_all[:, 2 * e0 : 2 * (e0 + count), :])
+        def load_w1(e0, count, tag):
+            t = keep.tile([P, 2 * count, 2 * H], U8, name=f"w1w{e0}", tag=tag, align_bytes=64)
+            nc.sync.dma_start(t[:].bitcast(I32), w1_all[:, 2 * e0 : 2 * (e0 + count), :])
             for i in range(count):
-                w1w[e0 + i] = [t[:, 2 * (at + i) + o, :] for o in range(2)]
+                w1w[e0 + i] = [t[:, 2 * i + o, :] for o in range(2)]
 
-        def load_planes(eng, dst, src):
+        def load_planes(dst, src):
             for q in range(4):
-                eng.dma_start(dst[32 * q : 32 * q + 4].bitcast(I32), src[:, 4 * q : 4 * q + 4, :].rearrange("a r n -> r a n").bitcast(I32))
+                nc.sync.dma_start(dst[32 * q : 32 * q + 4].bitcast(I32), src[:, 4 * q : 4 * q + 4, :].rearrange("a r n -> r a n").bitcast(I32))
 
         gw, gs = {}, {}
 
-        def gather(e):
-            slots = offs_sb[:, 16 * e : 16 * (e + 1)]
+        def gather_scales(e):
             for o in range(2):
-                gs[e, o] = ring.tile([P, C], U8, name=f"gs{o}", align_bytes=64, bufs=2)
-                nc.vector.tensor_copy(gs[e, o][:], xs[:, o, :].indirect(slots))
+                gs[e, o] = ring.tile([P, C], U8, name=f"gs{o}", align_bytes=64, bufs=3)
+                nc.vector.tensor_copy(gs[e, o][:], xs[:, o, :].indirect(offs_sb[:, 16 * e : 16 * (e + 1)]))
+
+        def gather_words(e):
             for o in range(2):
                 gw[e, o] = ring.tile([P, C], U32, name=f"gw{o}", align_bytes=64, bufs=2)
-                nc.vector.tensor_copy(gw[e, o][:], xw[o][:].bitcast(U32).indirect(slots))
+                nc.vector.tensor_copy(gw[e, o][:], xw[o][:].bitcast(U32).indirect(offs_sb[:, 16 * e : 16 * (e + 1)]))
 
-        w1s_all = w1_scales.rearrange("e s q n -> (e s) q n")
-        w_shared = keep.tile([P, 2, 2 * H], U8, name="w_shared", tag="w_shared", align_bytes=64)
-        w_mid = keep.tile([P, 8, 2 * H], U8, name="w_mid", tag="w_mid", align_bytes=64)
         nc.sync.dma_start(offs_sb[:], offs)
-        load_planes(nc.sync, xs, x_scales)
+        load_planes(xs, x_scales)
         nc.sync.dma_start(pos_sb[0][:], pos1)
         nc.sync.dma_start(pos_sb[1][:], pos2)
         for o in range(2):
             nc.sync.dma_start(xw[o][:], x_words[o].rearrange("p t r -> p (t r)").bitcast(I32))
-        load_planes(nc.sync, w1s_hi, w1s_all[8:14])
-        load_w1(w_shared, 0, 6, 1)
-        load_w1(w_mid, 2, 4, 2)
-        load_planes(nc.sync, w1s_lo, w1s_all[0:8])
-        load_w1(w_mid, 0, 2, 2)
-        load_planes(nc.sync, w2s, w2_scales.rearrange("e s q n -> (e s) q n"))
+        w1s_all = w1_scales.rearrange("e s q n -> (e s) q n")
+        load_planes(w1s_hi, w1s_all[8:14])
+        load_w1(6, 1, "w6")
+        load_w1(2, 4, "w2345")
+        load_planes(w1s_lo, w1s_all[0:8])
 
         def w1_plane(e, o):
             return w1s_hi[:, 2 * (e - 4) + o, :] if e >= 4 else w1s_lo[:, 2 * e + o, :]
@@ -106,49 +101,63 @@ def tile_moe_shr_mlp_gelu_kernel(tc, x_words, x_scales, w1_words, w1_scales, w2_
             cols = slice(g * C + j * P, g * C + (j + 1) * P)
             return xw[o][:, cols], xs[:, o, cols]
 
-        def hidden(step, e, operands, bank, copy_out, tags=None, cols_tag=None):
-            tb = bank[:].rearrange("p (j u s) -> p j u s", j=2, u=2)
-            halves = []
-            for j in range(2):
-                a = acc[(2 * step + j) % 3]
-                for o in range(2):
-                    words, scales = operands(j, o)
-                    nc.tensor.matmul_mx(a[:], lhsT=words.bitcast(FP8X4), lhsT_scale=scales, rhs=w1w[e][o].bitcast(FP4X4), rhs_scale=w1_plane(e, o), start=(o == 0), stop=(o == 1))
-                if tags:
-                    h_rows = keep.tile([P, H], BF16, name="h_first", tag=tags[j], align_bytes=64)
-                else:
-                    h_rows = ring.tile([P, H], BF16, name="h_rows")
-                nc.scalar.activation(h_rows[:].rearrange("p (u m d) -> p u m d", u=2, d=2), a[:].rearrange("p (m u d) -> p u m d", u=2, d=2), GELU)
-                halves.append(h_rows)
-            for j in range(2):
-                for u in range(2):
-                    nc.tensor.transpose(tb[:, j, u, :], halves[j][:].bitcast(F32)[:, u * P : (u + 1) * P], ident[:])
-            if cols_tag:
-                h_cols = keep.tile([P, 4 * C], BF16, name="h_late", tag=cols_tag, align_bytes=64)
+        def hidden_rows(acc, e, operands, j, tag=None):
+            for o in range(2):
+                words, scales = operands(j, o)
+                nc.tensor.matmul_mx(banks[acc][:], lhsT=words.bitcast(FP8X4), lhsT_scale=scales, rhs=w1w[e][o].bitcast(FP4X4), rhs_scale=w1_plane(e, o), start=(o == 0), stop=(o == 1))
+            if tag:
+                h_rows = keep.tile([P, H], BF16, name="h_first", tag=tag, align_bytes=64)
             else:
-                h_cols = ring.tile([P, 4 * C], BF16, name="h_cols", align_bytes=64, bufs=7)
-            copy_out(h_cols[:].bitcast(F32).rearrange("p (j s u) -> p j s u", j=2, u=2), tb.rearrange("p j u s -> p j s u"))
+                h_rows = ring.tile([P, H], BF16, name="h_rows")
+            nc.scalar.activation(h_rows[:].rearrange("p (u m d) -> p u m d", u=2, d=2), banks[acc][:].rearrange("p (m u d) -> p u m d", u=2, d=2), GELU)
+            return h_rows
+
+        def turn(rows, bank, copy_out, cols_tag=None):
+            count = len(rows)
+            tb = banks[bank][:, 0 : count * C].rearrange("p (j u s) -> p j u s", j=count, u=2)
+            for j in range(count):
+                for u in range(2):
+                    nc.tensor.transpose(tb[:, j, u, :], rows[j][:].bitcast(F32)[:, u * P : (u + 1) * P], ident[:])
+            if cols_tag:
+                h_cols = keep.tile([P, count * H], BF16, name="h_late", tag=cols_tag, align_bytes=64)
+            else:
+                h_cols = ring.tile([P, count * H], BF16, name="h_cols", align_bytes=64, bufs=6)
+            copy_out(h_cols[:].bitcast(F32).rearrange("p (j s u) -> p j s u", j=count, u=2), tb.rearrange("p j u s -> p j s u"))
             return h_cols
+
+        def hidden(accs, e, operands, bank, copy_out, tags=(None, None), cols_tag=None):
+            return turn([hidden_rows(accs[j], e, operands, j, tags[j]) for j in range(2)], bank, copy_out, cols_tag)
 
         on_scalar, on_vector = nc.scalar.copy, nc.vector.tensor_copy
         h = {}
-        gather(ORDER[0])
-        gather(ORDER[1])
-        h[6] = hidden(0, E, lambda j, o: shared_operands(0, j, o), spare[0], on_scalar, ("w_last", "w2"))
-        w_last = keep.tile([P, 4, 2 * H], U8, name="w_last", tag="w_last", align_bytes=64)
-        load_w1(w_last, 0, 0, 2)
-        w2w = keep.tile([P, E + 1, 2 * N], U8, name="w2w", tag="w2", align_bytes=64)
-        nc.sync.dma_start(w2w[:].bitcast(I32), w2_words.rearrange("e s p b -> p (e s) b").bitcast(I32))
-        turn = {4: spare[1], 5: spare[0], 2: spare[1], 3: spare[2], 0: spare[3], 1: spare[0]}
-        for n, e in enumerate(ORDER):
-            h[e] = hidden(n + 1, e, lambda j, o: routed_operands(e, j, o), turn[e], on_scalar if n < 4 else on_vector, ("gate", "gate2") if n == 0 else None)
+        for e in ORDER[:2]:
+            gather_scales(e)
+            gather_words(e)
+        gather_scales(ORDER[2])
+        h[6] = hidden((0, 1), E, lambda j, o: shared_operands(0, j, o), 3, on_scalar, ("w01", "w2s"))
+        load_w1(0, 2, "w01")
+        w2s = keep.tile([P, E + 1, N], U8, name="w2s", tag="w2s", align_bytes=64)
+        nc.gpsimd.memset(flat(w2s), 0)
+        load_planes(w2s, w2_scales.rearrange("e s q n -> (e s) q n"))
+        for n, e in enumerate(ORDER[:5]):
+            accs = ((2 * n + 2) % 3, (2 * n + 3) % 3)
+            h[e] = hidden(accs, e, lambda j, o: routed_operands(e, j, o), 4 - n % 2, on_vector if n in (4,) else on_scalar, ("w2", "gate") if n == 0 else (None, None))
             if n + 2 < E:
-                gather(ORDER[n + 2])
+                gather_words(ORDER[n + 2])
+            if n + 3 < E:
+                gather_scales(ORDER[n + 3])
             if n == 0:
+                w2w = keep.tile([P, E + 1, 2 * N], U8, name="w2w", tag="w2", align_bytes=64)
+                nc.sync.dma_start(w2w[:].bitcast(I32), w2_words.rearrange("e s p b -> p (e s) b").bitcast(I32))
                 gate_sb = keep.tile([P, 2, T], F32, name="gate_sb", tag="gate", align_bytes=64)
                 nc.sync.dma_start(gate_sb[:], gate.rearrange("r n t -> n r t"))
 
-        codes = keep.tile([P, 9, C], U32, name="codes", tag="w_mid", align_bytes=64)
+        last = []
+        for j in range(2):
+            rows = hidden_rows(j, 0, lambda j, o: routed_operands(0, j, o), j)
+            last.append(turn([rows], (3, 2)[j], on_vector, f"last{j}"))
+
+        codes = keep.tile([P, 9, C], U32, name="codes", tag="w2345", align_bytes=64)
 
         def quantise(u):
             nc.vector.quantize_mx(out=codes[:, u, :].bitcast(FP8X4), scales=planes[:, u, :], in_=h[u][:])
@@ -157,21 +166,24 @@ def tile_moe_shr_mlp_gelu_kernel(tc, x_words, x_scales, w1_words, w1_scales, w2_
             e = min(u, E)
             nc.tensor.matmul_mx(dst, lhsT=w2w[:, e, :].bitcast(FP4X4), lhsT_scale=w2s[:, e, :], rhs=codes[:, u, :].bitcast(FP8X4), rhs_scale=planes[:, u, :], start=True, stop=True)
 
-        for c, bank in ((2, spare[2]), (1, spare[3])):
-            for e in (2 * c, 2 * c + 1):
+        for c, bank in ((2, banks[0]), (1, banks[1])):
+            for e in (2 * c + 1, 2 * c):
                 quantise(e)
                 second(e, bank[:, (e % 2) * C : (e % 2 + 1) * C])
             nc.scalar.copy(y_sb[:, c * PAIR : (c + 1) * PAIR], bank[:])
-        for e in (0, 1):
-            quantise(e)
-            bank = (spare[4], spare[1])[e]
-            second(e, bank[:, 0:C])
-            (on_scalar, on_vector)[e](y_sb[:, e * C : (e + 1) * C], bank[:, 0:C])
-        ys = [spare[2][:, 0:C], spare[3][:, 0:C], spare[4][:, 0:C]]
+        quantise(1)
+        second(1, banks[5][:, 0:C])
+        nc.scalar.copy(y_sb[:, C : 2 * C], banks[5][:, 0:C])
+        for j in range(2):
+            cols = slice(j * P, (j + 1) * P)
+            nc.vector.quantize_mx(out=codes[:, 0, cols].bitcast(FP8X4), scales=planes[:, 0, cols], in_=last[j][:])
+            nc.tensor.matmul_mx(banks[6 + j][:, 0:P], lhsT=w2w[:, 0, :].bitcast(FP4X4), lhsT_scale=w2s[:, 0, :], rhs=codes[:, 0, cols].bitcast(FP8X4), rhs_scale=planes[:, 0, cols], start=True, stop=True)
+            nc.vector.tensor_copy(y_sb[:, cols], banks[6 + j][:, 0:P])
+        ys = [banks[3][:, 0:C], banks[6][:, 0:C], banks[7][:, 0:C]]
         quantise(6)
         second(6, ys[0])
         for g in (1, 2):
-            h[6 + g] = hidden(6 + g, E, lambda j, o: shared_operands(g, j, o), spare[g - 1], on_scalar, None, f"late{g}")
+            h[6 + g] = hidden(((0, 1), (5, 0))[g - 1], E, lambda j, o: shared_operands(g, j, o), (4, 2)[g - 1], on_scalar, (None, None), f"late{g}")
             quantise(6 + g)
             second(6 + g, ys[g])
 
@@ -179,10 +191,8 @@ def tile_moe_shr_mlp_gelu_kernel(tc, x_words, x_scales, w1_words, w1_scales, w2_
             tok = slice(g * C, (g + 1) * C)
             parts = []
             for r in range(2):
-                if r == 0:
-                    part = keep.tile([P, C], F32, name="part0", tag=f"late{g}", align_bytes=64)
-                else:
-                    part = keep.tile([P, C], F32, name="part1")
+                tag = ("free0", "late%d" % g)[r]
+                part = keep.tile([P, C], F32, name="part", tag=tag, align_bytes=64)
                 nc.vector.tensor_tensor(part[:], y_sb[:].indirect(pos_sb[r][:, 16 * g : 16 * (g + 1)]), gate_sb[:, r, tok], MULT)
                 parts.append(part)
             partial = ring.tile([P, C], F32, name="partial")

@@ -38,8 +38,8 @@ def tile_moe_shr_mlp_gelu_kernel(tc, x_words, x_scales, w1_words, w1_scales, w2_
         w1s_hi = keep.tile([P, 6, H], U8, name="w1s_hi", align_bytes=64)
         w1s_lo = keep.tile([P, 8, H], U8, name="w1s_lo", align_bytes=64)
         ident = keep.tile([P, P], F32, name="ident")
-        warm_in = keep.tile([P, 1], F32, name="warm_in", tag="w6", align_bytes=64)
-        warm_out = keep.tile([P, 1], F32, name="warm_out", tag="w2345", align_bytes=64)
+        warm_in = keep.tile([P, 1], F32, name="warm_in", tag="w56", align_bytes=64)
+        warm_out = keep.tile([P, 1], F32, name="warm_out", tag="w234", align_bytes=64)
         y_sb = keep.tile([P, S], F32, name="y_sb")
         planes = keep.tile([P, 9, C], U8, name="planes", align_bytes=64)
         banks = [psum.tile([P, H], F32, name=f"bank{b}") for b in range(8)]
@@ -76,7 +76,7 @@ def tile_moe_shr_mlp_gelu_kernel(tc, x_words, x_scales, w1_words, w1_scales, w2_
 
         def gather_words(e):
             for o in range(2):
-                gw[e, o] = ring.tile([P, C], U32, name=f"gw{o}", align_bytes=64, bufs=2)
+                gw[e, o] = ring.tile([P, C], U32, name=f"gw{o}", align_bytes=64, bufs=3)
                 nc.vector.tensor_copy(gw[e, o][:], xw[o][:].bitcast(U32).indirect(offs_sb[:, 16 * e : 16 * (e + 1)]))
 
         nc.sync.dma_start(offs_sb[:], offs)
@@ -87,8 +87,8 @@ def tile_moe_shr_mlp_gelu_kernel(tc, x_words, x_scales, w1_words, w1_scales, w2_
             nc.sync.dma_start(xw[o][:], x_words[o].rearrange("p t r -> p (t r)").bitcast(I32))
         w1s_all = w1_scales.rearrange("e s q n -> (e s) q n")
         load_planes(w1s_hi, w1s_all[8:14])
-        load_w1(6, 1, "w6")
-        load_w1(2, 4, "w2345")
+        load_w1(5, 2, "w56")
+        load_w1(2, 3, "w234")
         load_planes(w1s_lo, w1s_all[0:8])
 
         def w1_plane(e, o):
@@ -130,10 +130,9 @@ def tile_moe_shr_mlp_gelu_kernel(tc, x_words, x_scales, w1_words, w1_scales, w2_
 
         on_scalar, on_vector = nc.scalar.copy, nc.vector.tensor_copy
         h = {}
-        for e in ORDER[:2]:
+        for e in ORDER[:3]:
             gather_scales(e)
             gather_words(e)
-        gather_scales(ORDER[2])
         h[6] = hidden((0, 1), E, lambda j, o: shared_operands(0, j, o), 3, on_scalar, ("w01", "w2s"))
         load_w1(0, 2, "w01")
         w2s = keep.tile([P, E + 1, N], U8, name="w2s", tag="w2s", align_bytes=64)
@@ -142,10 +141,9 @@ def tile_moe_shr_mlp_gelu_kernel(tc, x_words, x_scales, w1_words, w1_scales, w2_
         for n, e in enumerate(ORDER[:5]):
             accs = ((2 * n + 2) % 3, (2 * n + 3) % 3)
             h[e] = hidden(accs, e, lambda j, o: routed_operands(e, j, o), 4 - n % 2, on_vector if n in (4,) else on_scalar, ("w2", "gate") if n == 0 else (None, None))
-            if n + 2 < E:
-                gather_words(ORDER[n + 2])
             if n + 3 < E:
                 gather_scales(ORDER[n + 3])
+                gather_words(ORDER[n + 3])
             if n == 0:
                 w2w = keep.tile([P, E + 1, 2 * N], U8, name="w2w", tag="w2", align_bytes=64)
                 nc.sync.dma_start(w2w[:].bitcast(I32), w2_words.rearrange("e s p b -> p (e s) b").bitcast(I32))
@@ -157,7 +155,7 @@ def tile_moe_shr_mlp_gelu_kernel(tc, x_words, x_scales, w1_words, w1_scales, w2_
             rows = hidden_rows(j, 0, lambda j, o: routed_operands(0, j, o), j)
             last.append(turn([rows], (3, 2)[j], on_vector, f"last{j}"))
 
-        codes = keep.tile([P, 9, C], U32, name="codes", tag="w2345", align_bytes=64)
+        codes = keep.tile([P, 9, C], U32, name="codes", tag="w234", align_bytes=64)
 
         def quantise(u):
             nc.vector.quantize_mx(out=codes[:, u, :].bitcast(FP8X4), scales=planes[:, u, :], in_=h[u][:])

@@ -19,9 +19,16 @@ MULT = mybir.AluOpType.mult
 ADD = mybir.AluOpType.add
 
 P = 128
-S = E * C
-PAIR = 2 * C
-ORDER = (5, 4, 3, 2, 1, 0)
+PASSES = K // 512
+PER_COLUMN = 16
+SLOTS = E * C
+SHARED = E
+THIRDS = T // C
+ORDER = tuple(reversed(range(E)))
+AHEAD = 3
+ACC_BANKS = 3
+TURN_BANKS = (3, 4)
+FIRST_HI = 4
 
 
 def tile_moe_shr_mlp_gelu_kernel(tc, x_words, x_scales, w1_words, w1_scales, w2_words, w2_scales, gate, offs, pos1, pos2, out):
@@ -31,170 +38,162 @@ def tile_moe_shr_mlp_gelu_kernel(tc, x_words, x_scales, w1_words, w1_scales, w2_
         ring = ctx.enter_context(tc.tile_pool(name="ring", bufs=4))
         psum = ctx.enter_context(tc.psum_pool(name="psum", bufs=1))
 
-        offs_sb = keep.tile([P, S // 16], U16, name="offs_sb")
-        pos_sb = [keep.tile([P, T // 16], U16, name=f"pos{r}_sb") for r in range(2)]
-        xw = [keep.tile([P, T], I32, name=f"xw{o}", align_bytes=64) for o in range(2)]
-        xs = keep.tile([P, 2, T], U8, name="xs", align_bytes=64)
-        w1s_hi = keep.tile([P, 6, H], U8, name="w1s_hi", align_bytes=64)
-        w1s_lo = keep.tile([P, 8, H], U8, name="w1s_lo", align_bytes=64)
+        offs_sb = keep.tile([P, SLOTS // PER_COLUMN], U16, name="offs_sb")
+        pos_sb = [keep.tile([P, T // PER_COLUMN], U16, name=f"pos{r}_sb") for r in range(2)]
+        xw = [keep.tile([P, T], I32, name=f"xw{o}", align_bytes=64) for o in range(PASSES)]
+        xs = keep.tile([P, PASSES, T], U8, name="xs", align_bytes=64)
+        w1s_hi = keep.tile([P, PASSES * (E + 1 - FIRST_HI), H], U8, name="w1s_hi", align_bytes=64)
+        w1s_lo = keep.tile([P, PASSES * FIRST_HI, H], U8, name="w1s_lo", align_bytes=64)
         ident = keep.tile([P, P], F32, name="ident")
         warm_in = keep.tile([P, 1], F32, name="warm_in", tag="w56", align_bytes=64)
         warm_out = keep.tile([P, 1], F32, name="warm_out", tag="w234", align_bytes=64)
-        y_sb = keep.tile([P, S], F32, name="y_sb")
-        planes = keep.tile([P, 9, C], U8, name="planes", align_bytes=64)
+        y_sb = keep.tile([P, SLOTS], F32, name="y_sb")
+        planes = keep.tile([P, E + THIRDS, C], U8, name="planes", align_bytes=64)
         banks = [psum.tile([P, H], F32, name=f"bank{b}") for b in range(8)]
 
-        def flat(t):
-            return t[:].rearrange("p a b -> p (a b)").bitcast(I32)
+        def as_int32(plane_tile):
+            return plane_tile[:].rearrange("p a b -> p (a b)").bitcast(I32)
 
-        nc.vector.memset(flat(xs), 0)
+        nc.vector.memset(as_int32(xs), 0)
         nc.gpsimd.memset(warm_in[:], 0.0)
         nc.scalar.activation(warm_out[:], warm_in[:], GELU)
-        nc.vector.memset(flat(w1s_hi), 0)
+        nc.vector.memset(as_int32(w1s_hi), 0)
         make_identity(nc, ident[:])
-        nc.gpsimd.memset(flat(w1s_lo), 0)
+        nc.gpsimd.memset(as_int32(w1s_lo), 0)
 
         w1_all = w1_words.rearrange("e s p b -> p (e s) b").bitcast(I32)
         w1w = {}
 
-        def load_w1(e0, count, tag):
-            t = keep.tile([P, 2 * count, 2 * H], U8, name=f"w1w{e0}", tag=tag, align_bytes=64)
-            nc.sync.dma_start(t[:].bitcast(I32), w1_all[:, 2 * e0 : 2 * (e0 + count), :])
+        def load_w1(first, count, tag):
+            words = keep.tile([P, PASSES * count, 2 * H], U8, name=f"w1w{first}", tag=tag, align_bytes=64)
+            nc.sync.dma_start(words[:].bitcast(I32), w1_all[:, PASSES * first : PASSES * (first + count), :])
             for i in range(count):
-                w1w[e0 + i] = [t[:, 2 * i + o, :] for o in range(2)]
+                w1w[first + i] = [words[:, PASSES * i + o, :] for o in range(PASSES)]
 
         def load_planes(dst, src):
             for q in range(4):
                 nc.sync.dma_start(dst[32 * q : 32 * q + 4].bitcast(I32), src[:, 4 * q : 4 * q + 4, :].rearrange("a r n -> r a n").bitcast(I32))
 
-        gw, gs = {}, {}
+        gathered_words, gathered_scales = {}, {}
 
-        def gather_scales(e):
-            for o in range(2):
-                gs[e, o] = ring.tile([P, C], U8, name=f"gs{o}", align_bytes=64, bufs=3)
-                nc.vector.tensor_copy(gs[e, o][:], xs[:, o, :].indirect(offs_sb[:, 16 * e : 16 * (e + 1)]))
+        def gather(e):
+            slots = offs_sb[:, e * C // PER_COLUMN : (e + 1) * C // PER_COLUMN]
+            for o in range(PASSES):
+                gathered_scales[e, o] = ring.tile([P, C], U8, name=f"gs{o}", align_bytes=64, bufs=AHEAD)
+                nc.vector.tensor_copy(gathered_scales[e, o][:], xs[:, o, :].indirect(slots))
+            for o in range(PASSES):
+                gathered_words[e, o] = ring.tile([P, C], U32, name=f"gw{o}", align_bytes=64, bufs=AHEAD)
+                nc.vector.tensor_copy(gathered_words[e, o][:], xw[o][:].bitcast(U32).indirect(slots))
 
-        def gather_words(e):
-            for o in range(2):
-                gw[e, o] = ring.tile([P, C], U32, name=f"gw{o}", align_bytes=64, bufs=3)
-                nc.vector.tensor_copy(gw[e, o][:], xw[o][:].bitcast(U32).indirect(offs_sb[:, 16 * e : 16 * (e + 1)]))
-
+        w1s_all = w1_scales.rearrange("e s q n -> (e s) q n")
         nc.sync.dma_start(offs_sb[:], offs)
         load_planes(xs, x_scales)
         nc.sync.dma_start(pos_sb[0][:], pos1)
         nc.sync.dma_start(pos_sb[1][:], pos2)
-        for o in range(2):
+        for o in range(PASSES):
             nc.sync.dma_start(xw[o][:], x_words[o].rearrange("p t r -> p (t r)").bitcast(I32))
-        w1s_all = w1_scales.rearrange("e s q n -> (e s) q n")
-        load_planes(w1s_hi, w1s_all[8:14])
+        load_planes(w1s_hi, w1s_all[PASSES * FIRST_HI :])
         load_w1(5, 2, "w56")
         load_w1(2, 3, "w234")
-        load_planes(w1s_lo, w1s_all[0:8])
+        load_planes(w1s_lo, w1s_all[: PASSES * FIRST_HI])
 
         def w1_plane(e, o):
-            return w1s_hi[:, 2 * (e - 4) + o, :] if e >= 4 else w1s_lo[:, 2 * e + o, :]
+            return w1s_hi[:, PASSES * (e - FIRST_HI) + o, :] if e >= FIRST_HI else w1s_lo[:, PASSES * e + o, :]
 
-        def routed_operands(e, j, o):
-            return gw[e, o][:, j * P : (j + 1) * P], gs[e, o][:, j * P : (j + 1) * P]
-
-        def shared_operands(g, j, o):
-            cols = slice(g * C + j * P, g * C + (j + 1) * P)
+        def token_operands(unit, j, o):
+            if unit < SHARED:
+                cols = slice(j * P, (j + 1) * P)
+                return gathered_words[unit, o][:, cols], gathered_scales[unit, o][:, cols]
+            cols = slice((unit - SHARED) * C + j * P, (unit - SHARED) * C + (j + 1) * P)
             return xw[o][:, cols], xs[:, o, cols]
 
-        def hidden_rows(acc, e, operands, j, tag=None):
-            for o in range(2):
-                words, scales = operands(j, o)
-                nc.tensor.matmul_mx(banks[acc][:], lhsT=words.bitcast(FP8X4), lhsT_scale=scales, rhs=w1w[e][o].bitcast(FP4X4), rhs_scale=w1_plane(e, o), start=(o == 0), stop=(o == 1))
-            if tag:
-                h_rows = keep.tile([P, H], BF16, name="h_first", tag=tag, align_bytes=64)
-            else:
-                h_rows = ring.tile([P, H], BF16, name="h_rows")
-            nc.scalar.activation(h_rows[:].rearrange("p (u m d) -> p u m d", u=2, d=2), banks[acc][:].rearrange("p (m u d) -> p u m d", u=2, d=2), GELU)
+        def hidden_rows(unit, j, acc, h_rows):
+            e = min(unit, SHARED)
+            for o in range(PASSES):
+                words, scales = token_operands(unit, j, o)
+                nc.tensor.matmul_mx(banks[acc][:], lhsT=words.bitcast(FP8X4), lhsT_scale=scales, rhs=w1w[e][o].bitcast(FP4X4), rhs_scale=w1_plane(e, o), start=(o == 0), stop=(o == PASSES - 1))
+            nc.scalar.activation(h_rows.rearrange("p (u m d) -> p u m d", u=2, d=2), banks[acc][:].rearrange("p (m u d) -> p u m d", u=2, d=2), GELU)
             return h_rows
 
-        def turn(rows, bank, copy_out, cols_tag=None):
+        def turn(rows, bank, copy_out, tag=None):
             count = len(rows)
-            tb = banks[bank][:, 0 : count * C].rearrange("p (j u s) -> p j u s", j=count, u=2)
+            turned = banks[bank][:, 0 : count * 2 * P].rearrange("p (j u s) -> p j u s", j=count, u=2)
             for j in range(count):
                 for u in range(2):
-                    nc.tensor.transpose(tb[:, j, u, :], rows[j][:].bitcast(F32)[:, u * P : (u + 1) * P], ident[:])
-            if cols_tag:
-                h_cols = keep.tile([P, count * H], BF16, name="h_late", tag=cols_tag, align_bytes=64)
+                    nc.tensor.transpose(turned[:, j, u, :], rows[j].bitcast(F32)[:, u * P : (u + 1) * P], ident[:])
+            if tag:
+                h_cols = keep.tile([P, count * 4 * P], BF16, name="h_cols_tagged", tag=tag, align_bytes=64)
             else:
-                h_cols = ring.tile([P, count * H], BF16, name="h_cols", align_bytes=64, bufs=6)
-            copy_out(h_cols[:].bitcast(F32).rearrange("p (j s u) -> p j s u", j=count, u=2), tb.rearrange("p j u s -> p j s u"))
+                h_cols = ring.tile([P, count * 4 * P], BF16, name="h_cols", align_bytes=64, bufs=6)
+            copy_out(h_cols[:].bitcast(F32).rearrange("p (j s u) -> p j s u", j=count, u=2), turned.rearrange("p j u s -> p j s u"))
             return h_cols
 
-        def hidden(accs, e, operands, bank, copy_out, tags=(None, None), cols_tag=None):
-            return turn([hidden_rows(accs[j], e, operands, j, tags[j]) for j in range(2)], bank, copy_out, cols_tag)
+        def hidden(unit, accs, bank, copy_out, row_tag=None, col_tag=None):
+            if row_tag:
+                both = keep.tile([P, 2, H], BF16, name="h_rows_tagged", tag=row_tag, align_bytes=64)
+            else:
+                both = ring.tile([P, 2, H], BF16, name="h_rows")
+            return turn([hidden_rows(unit, j, accs[j], both[:, j, :]) for j in range(2)], bank, copy_out, col_tag)
 
-        on_scalar, on_vector = nc.scalar.copy, nc.vector.tensor_copy
+        def in_turn(step):
+            return ((2 * step) % ACC_BANKS, (2 * step + 1) % ACC_BANKS)
+
+        late_tags = ("w01", "w2s", "w2", "gate")
         h = {}
-        for e in ORDER[:3]:
-            gather_scales(e)
-            gather_words(e)
-        h[6] = hidden((0, 1), E, lambda j, o: shared_operands(0, j, o), 3, on_scalar, ("w01", "w2s"))
+        for e in ORDER[:AHEAD]:
+            gather(e)
+        h[SHARED] = hidden(SHARED, in_turn(0), TURN_BANKS[0], nc.scalar.copy, late_tags[0])
         load_w1(0, 2, "w01")
+        for step, e in enumerate(ORDER[:-1], 1):
+            copy_out = nc.vector.tensor_copy if e == 1 else nc.scalar.copy
+            h[e] = hidden(e, in_turn(step), TURN_BANKS[step % 2], copy_out, late_tags[step] if step < len(late_tags) else None)
+            if step - 1 + AHEAD < E:
+                gather(ORDER[step - 1 + AHEAD])
         w2s = keep.tile([P, E + 1, N], U8, name="w2s", tag="w2s", align_bytes=64)
-        nc.gpsimd.memset(flat(w2s), 0)
+        nc.gpsimd.memset(as_int32(w2s), 0)
         load_planes(w2s, w2_scales.rearrange("e s q n -> (e s) q n"))
-        for n, e in enumerate(ORDER[:5]):
-            accs = ((2 * n + 2) % 3, (2 * n + 3) % 3)
-            h[e] = hidden(accs, e, lambda j, o: routed_operands(e, j, o), 4 - n % 2, on_vector if n in (4,) else on_scalar, ("w2", "gate") if n == 0 else (None, None))
-            if n + 3 < E:
-                gather_scales(ORDER[n + 3])
-                gather_words(ORDER[n + 3])
-            if n == 0:
-                w2w = keep.tile([P, E + 1, 2 * N], U8, name="w2w", tag="w2", align_bytes=64)
-                nc.sync.dma_start(w2w[:].bitcast(I32), w2_words.rearrange("e s p b -> p (e s) b").bitcast(I32))
-                gate_sb = keep.tile([P, 2, T], F32, name="gate_sb", tag="gate", align_bytes=64)
-                nc.sync.dma_start(gate_sb[:], gate.rearrange("r n t -> n r t"))
+        w2w = keep.tile([P, E + 1, 2 * N], U8, name="w2w", tag="w2", align_bytes=64)
+        nc.sync.dma_start(w2w[:].bitcast(I32), w2_words.rearrange("e s p b -> p (e s) b").bitcast(I32))
+        gate_sb = keep.tile([P, 2, T], F32, name="gate_sb", tag="gate", align_bytes=64)
+        nc.sync.dma_start(gate_sb[:], gate.rearrange("r n t -> n r t"))
 
         last = []
-        for j in range(2):
-            rows = hidden_rows(j, 0, lambda j, o: routed_operands(0, j, o), j)
-            last.append(turn([rows], (3, 2)[j], on_vector, f"last{j}"))
+        for j, acc in enumerate(in_turn(E)):
+            h_rows = keep.tile([P, H], BF16, name=f"last_rows{j}")
+            last.append(turn([hidden_rows(0, j, acc, h_rows[:])], (3, 2)[j], nc.vector.tensor_copy, f"last{j}"))
 
-        codes = keep.tile([P, 9, C], U32, name="codes", tag="w234", align_bytes=64)
+        codes = keep.tile([P, E + THIRDS, C], U32, name="codes", tag="w234", align_bytes=64)
 
-        def quantise(u):
-            nc.vector.quantize_mx(out=codes[:, u, :].bitcast(FP8X4), scales=planes[:, u, :], in_=h[u][:])
+        def second(e, words, scales, h_cols, dst):
+            nc.vector.quantize_mx(out=words.bitcast(FP8X4), scales=scales, in_=h_cols[:])
+            nc.tensor.matmul_mx(dst, lhsT=w2w[:, e, :].bitcast(FP4X4), lhsT_scale=w2s[:, e, :], rhs=words.bitcast(FP8X4), rhs_scale=scales, start=True, stop=True)
 
-        def second(u, dst):
-            e = min(u, E)
-            nc.tensor.matmul_mx(dst, lhsT=w2w[:, e, :].bitcast(FP4X4), lhsT_scale=w2s[:, e, :], rhs=codes[:, u, :].bitcast(FP8X4), rhs_scale=planes[:, u, :], start=True, stop=True)
-
-        for c, bank in ((2, banks[0]), (1, banks[1])):
-            for e in (2 * c + 1, 2 * c):
-                quantise(e)
-                second(e, bank[:, (e % 2) * C : (e % 2 + 1) * C])
-            nc.scalar.copy(y_sb[:, c * PAIR : (c + 1) * PAIR], bank[:])
-        quantise(1)
-        second(1, banks[5][:, 0:C])
-        nc.scalar.copy(y_sb[:, C : 2 * C], banks[5][:, 0:C])
+        for experts, bank in (((5, 4), 0), ((3, 2), 1), ((1,), 5)):
+            low = experts[-1]
+            for e in experts:
+                second(e, codes[:, e, :], planes[:, e, :], h[e], banks[bank][:, (e - low) * C : (e - low + 1) * C])
+            nc.scalar.copy(y_sb[:, low * C : (low + len(experts)) * C], banks[bank][:, 0 : len(experts) * C])
         for j in range(2):
             cols = slice(j * P, (j + 1) * P)
-            nc.vector.quantize_mx(out=codes[:, 0, cols].bitcast(FP8X4), scales=planes[:, 0, cols], in_=last[j][:])
-            nc.tensor.matmul_mx(banks[6 + j][:, 0:P], lhsT=w2w[:, 0, :].bitcast(FP4X4), lhsT_scale=w2s[:, 0, :], rhs=codes[:, 0, cols].bitcast(FP8X4), rhs_scale=planes[:, 0, cols], start=True, stop=True)
-            nc.vector.tensor_copy(y_sb[:, cols], banks[6 + j][:, 0:P])
-        ys = [banks[3][:, 0:C], banks[6][:, 0:C], banks[7][:, 0:C]]
-        quantise(6)
-        second(6, ys[0])
-        for g in (1, 2):
-            h[6 + g] = hidden(((0, 1), (5, 0))[g - 1], E, lambda j, o: shared_operands(g, j, o), (4, 2)[g - 1], on_scalar, (None, None), f"late{g}")
-            quantise(6 + g)
-            second(6 + g, ys[g])
+            second(0, codes[:, 0, cols], planes[:, 0, cols], last[j], banks[6][:, cols])
+        nc.vector.tensor_copy(y_sb[:, 0:C], banks[6][:, 0:C])
 
-        for g in range(3):
-            tok = slice(g * C, (g + 1) * C)
+        ys = [banks[b][:, 0:C] for b in (3, 6, 7)]
+        first_codes = keep.tile([P, C], U32, name="first_codes", tag="last1", align_bytes=64)
+        second(SHARED, first_codes[:], planes[:, SHARED, :], h[SHARED], ys[0])
+        for third, accs, bank in ((1, (0, 1), 4), (2, (5, 0), 2)):
+            unit = SHARED + third
+            second(SHARED, codes[:, unit, :], planes[:, unit, :], hidden(unit, accs, bank, nc.scalar.copy, col_tag=f"third{third}"), ys[third])
+
+        for third in range(THIRDS):
+            tok = slice(third * C, (third + 1) * C)
             parts = []
-            for r in range(2):
-                tag = ("free0", "late%d" % g)[r]
+            for r, tag in enumerate(("part", f"third{third}")):
                 part = keep.tile([P, C], F32, name="part", tag=tag, align_bytes=64)
-                nc.vector.tensor_tensor(part[:], y_sb[:].indirect(pos_sb[r][:, 16 * g : 16 * (g + 1)]), gate_sb[:, r, tok], MULT)
+                nc.vector.tensor_tensor(part[:], y_sb[:].indirect(pos_sb[r][:, third * C // PER_COLUMN : (third + 1) * C // PER_COLUMN]), gate_sb[:, r, tok], MULT)
                 parts.append(part)
             partial = ring.tile([P, C], F32, name="partial")
-            nc.vector.tensor_tensor(partial[:], parts[0][:], ys[g], ADD)
+            nc.vector.tensor_tensor(partial[:], parts[0][:], ys[third], ADD)
             total = ring.tile([P, C], F32, name="total")
             nc.vector.tensor_tensor(total[:], partial[:], parts[1][:], ADD)
             nc.sync.dma_start(out[:, tok], total[:])

from contextlib import ExitStack

import concourse.mybir as mybir
from concourse.masks import make_identity

K, T, E, C, H, N = 1024, 768, 6, 256, 512, 128
FLOPS = 2 * (E * C + T) * (K * H + H * N)

F32 = mybir.dt.float32
BF16 = mybir.dt.bfloat16
I32 = mybir.dt.int32
U32 = mybir.dt.uint32
U16 = mybir.dt.uint16
U8 = mybir.dt.uint8
FP8X4 = mybir.dt.float8_e4m3fn_x4
FP4X4 = mybir.dt.float4_e2m1fn_x4
GELU = mybir.ActivationFunctionType.Gelu_apprx_tanh
MULT = mybir.AluOpType.mult
ADD = mybir.AluOpType.add

P = 128
PASSES = K // 512
PER_COLUMN = 16
SLOTS = E * C
SHARED = E
THIRDS = T // C
ORDER = tuple(reversed(range(E)))
AHEAD = 3
ACC_BANKS = 3
TURN_BANKS = (3, 4)
FIRST_HI = 4


def tile_moe_shr_mlp_gelu_kernel(tc, x_words, x_scales, w1_words, w1_scales, w2_words, w2_scales, gate, offs, pos1, pos2, out):
    nc = tc.nc
    with ExitStack() as ctx:
        keep = ctx.enter_context(tc.tile_pool(name="keep", bufs=1))
        ring = ctx.enter_context(tc.tile_pool(name="ring", bufs=4))
        psum = ctx.enter_context(tc.psum_pool(name="psum", bufs=1))

        offs_sb = keep.tile([P, SLOTS // PER_COLUMN], U16, name="offs_sb")
        pos_sb = [keep.tile([P, T // PER_COLUMN], U16, name=f"pos{r}_sb") for r in range(2)]
        xw = [keep.tile([P, T], I32, name=f"xw{o}", align_bytes=64) for o in range(PASSES)]
        xs = keep.tile([P, PASSES, T], U8, name="xs", align_bytes=64)
        w1s_hi = keep.tile([P, PASSES * (E + 1 - FIRST_HI), H], U8, name="w1s_hi", align_bytes=64)
        w1s_lo = keep.tile([P, PASSES * FIRST_HI, H], U8, name="w1s_lo", align_bytes=64)
        ident = keep.tile([P, P], F32, name="ident")
        warm_in = keep.tile([P, 1], F32, name="warm_in", tag="w56", align_bytes=64)
        warm_out = keep.tile([P, 1], F32, name="warm_out", tag="w234", align_bytes=64)
        y_sb = keep.tile([P, SLOTS], F32, name="y_sb")
        planes = keep.tile([P, E + THIRDS, C], U8, name="planes", align_bytes=64)
        banks = [psum.tile([P, H], F32, name=f"bank{b}") for b in range(8)]

        def as_int32(plane_tile):
            return plane_tile[:].rearrange("p a b -> p (a b)").bitcast(I32)

        nc.vector.memset(as_int32(xs), 0)
        nc.gpsimd.memset(warm_in[:], 0.0)
        nc.scalar.activation(warm_out[:], warm_in[:], GELU)
        nc.vector.memset(as_int32(w1s_hi), 0)
        make_identity(nc, ident[:])
        nc.gpsimd.memset(as_int32(w1s_lo), 0)

        w1_all = w1_words.rearrange("e s p b -> p (e s) b").bitcast(I32)
        w1w = {}

        def load_w1(first, count, tag):
            words = keep.tile([P, PASSES * count, 2 * H], U8, name=f"w1w{first}", tag=tag, align_bytes=64)
            nc.sync.dma_start(words[:].bitcast(I32), w1_all[:, PASSES * first : PASSES * (first + count), :])
            for i in range(count):
                w1w[first + i] = [words[:, PASSES * i + o, :] for o in range(PASSES)]

        def load_planes(dst, src):
            for q in range(4):
                nc.sync.dma_start(dst[32 * q : 32 * q + 4].bitcast(I32), src[:, 4 * q : 4 * q + 4, :].rearrange("a r n -> r a n").bitcast(I32))

        gathered_words, gathered_scales = {}, {}

        def gather(e):
            slots = offs_sb[:, e * C // PER_COLUMN : (e + 1) * C // PER_COLUMN]
            for o in range(PASSES):
                gathered_scales[e, o] = ring.tile([P, C], U8, name=f"gs{o}", align_bytes=64, bufs=AHEAD)
                nc.vector.tensor_copy(gathered_scales[e, o][:], xs[:, o, :].indirect(slots))
            for o in range(PASSES):
                gathered_words[e, o] = ring.tile([P, C], U32, name=f"gw{o}", align_bytes=64, bufs=AHEAD)
                nc.vector.tensor_copy(gathered_words[e, o][:], xw[o][:].bitcast(U32).indirect(slots))

        w1s_all = w1_scales.rearrange("e s q n -> (e s) q n")
        nc.sync.dma_start(offs_sb[:], offs)
        load_planes(xs, x_scales)
        nc.sync.dma_start(pos_sb[0][:], pos1)
        nc.sync.dma_start(pos_sb[1][:], pos2)
        for o in range(PASSES):
            nc.sync.dma_start(xw[o][:], x_words[o].rearrange("p t r -> p (t r)").bitcast(I32))
        load_planes(w1s_hi, w1s_all[PASSES * FIRST_HI :])
        load_w1(5, 2, "w56")
        load_w1(2, 3, "w234")
        load_planes(w1s_lo, w1s_all[: PASSES * FIRST_HI])

        def w1_plane(e, o):
            return w1s_hi[:, PASSES * (e - FIRST_HI) + o, :] if e >= FIRST_HI else w1s_lo[:, PASSES * e + o, :]

        def token_operands(unit, j, o):
            if unit < SHARED:
                cols = slice(j * P, (j + 1) * P)
                return gathered_words[unit, o][:, cols], gathered_scales[unit, o][:, cols]
            cols = slice((unit - SHARED) * C + j * P, (unit - SHARED) * C + (j + 1) * P)
            return xw[o][:, cols], xs[:, o, cols]

        def hidden_rows(unit, j, acc, h_rows):
            e = min(unit, SHARED)
            for o in range(PASSES):
                words, scales = token_operands(unit, j, o)
                nc.tensor.matmul_mx(banks[acc][:], lhsT=words.bitcast(FP8X4), lhsT_scale=scales, rhs=w1w[e][o].bitcast(FP4X4), rhs_scale=w1_plane(e, o), start=(o == 0), stop=(o == PASSES - 1))
            nc.scalar.activation(h_rows.rearrange("p (u m d) -> p u m d", u=2, d=2), banks[acc][:].rearrange("p (m u d) -> p u m d", u=2, d=2), GELU)
            return h_rows

        def turn(rows, bank, copy_out, tag=None):
            count = len(rows)
            turned = banks[bank][:, 0 : count * 2 * P].rearrange("p (j u s) -> p j u s", j=count, u=2)
            for j in range(count):
                for u in range(2):
                    nc.tensor.transpose(turned[:, j, u, :], rows[j].bitcast(F32)[:, u * P : (u + 1) * P], ident[:])
            if tag:
                h_cols = keep.tile([P, count * 4 * P], BF16, name="h_cols_tagged", tag=tag, align_bytes=64)
            else:
                h_cols = ring.tile([P, count * 4 * P], BF16, name="h_cols", align_bytes=64, bufs=6)
            copy_out(h_cols[:].bitcast(F32).rearrange("p (j s u) -> p j s u", j=count, u=2), turned.rearrange("p j u s -> p j s u"))
            return h_cols

        def hidden(unit, accs, bank, copy_out, row_tag=None, col_tag=None):
            if row_tag:
                both = keep.tile([P, 2, H], BF16, name="h_rows_tagged", tag=row_tag, align_bytes=64)
            else:
                both = ring.tile([P, 2, H], BF16, name="h_rows")
            return turn([hidden_rows(unit, j, accs[j], both[:, j, :]) for j in range(2)], bank, copy_out, col_tag)

        def in_turn(step):
            return ((2 * step) % ACC_BANKS, (2 * step + 1) % ACC_BANKS)

        late_tags = ("w01", "w2s", "w2", "gate")
        h = {}
        for e in ORDER[:AHEAD]:
            gather(e)
        h[SHARED] = hidden(SHARED, in_turn(0), TURN_BANKS[0], nc.scalar.copy, late_tags[0])
        load_w1(0, 2, "w01")
        for step, e in enumerate(ORDER[:-1], 1):
            copy_out = nc.vector.tensor_copy if e == 1 else nc.scalar.copy
            h[e] = hidden(e, in_turn(step), TURN_BANKS[step % 2], copy_out, late_tags[step] if step < len(late_tags) else None)
            if step - 1 + AHEAD < E:
                gather(ORDER[step - 1 + AHEAD])
        w2s = keep.tile([P, E + 1, N], U8, name="w2s", tag="w2s", align_bytes=64)
        nc.gpsimd.memset(as_int32(w2s), 0)
        load_planes(w2s, w2_scales.rearrange("e s q n -> (e s) q n"))
        w2w = keep.tile([P, E + 1, 2 * N], U8, name="w2w", tag="w2", align_bytes=64)
        nc.sync.dma_start(w2w[:].bitcast(I32), w2_words.rearrange("e s p b -> p (e s) b").bitcast(I32))
        gate_sb = keep.tile([P, 2, T], F32, name="gate_sb", tag="gate", align_bytes=64)
        nc.sync.dma_start(gate_sb[:], gate.rearrange("r n t -> n r t"))

        last = []
        for j, acc in enumerate(in_turn(E)):
            h_rows = keep.tile([P, H], BF16, name=f"last_rows{j}")
            last.append(turn([hidden_rows(0, j, acc, h_rows[:])], (3, 2)[j], nc.vector.tensor_copy, f"last{j}"))

        codes = keep.tile([P, E + THIRDS, C], U32, name="codes", tag="w234", align_bytes=64)

        def second(e, words, scales, h_cols, dst):
            nc.vector.quantize_mx(out=words.bitcast(FP8X4), scales=scales, in_=h_cols[:])
            nc.tensor.matmul_mx(dst, lhsT=w2w[:, e, :].bitcast(FP4X4), lhsT_scale=w2s[:, e, :], rhs=words.bitcast(FP8X4), rhs_scale=scales, start=True, stop=True)

        for experts, bank in (((5, 4), 0), ((3, 2), 1), ((1,), 5)):
            low = experts[-1]
            for e in experts:
                second(e, codes[:, e, :], planes[:, e, :], h[e], banks[bank][:, (e - low) * C : (e - low + 1) * C])
            nc.scalar.copy(y_sb[:, low * C : (low + len(experts)) * C], banks[bank][:, 0 : len(experts) * C])
        for j in range(2):
            cols = slice(j * P, (j + 1) * P)
            second(0, codes[:, 0, cols], planes[:, 0, cols], last[j], banks[6][:, cols])
        nc.vector.tensor_copy(y_sb[:, 0:C], banks[6][:, 0:C])

        ys = [banks[b][:, 0:C] for b in (3, 6, 7)]
        first_codes = keep.tile([P, C], U32, name="first_codes", tag="last1", align_bytes=64)
        second(SHARED, first_codes[:], planes[:, SHARED, :], h[SHARED], ys[0])
        for third, accs, bank in ((1, (0, 1), 4), (2, (5, 0), 2)):
            unit = SHARED + third
            second(SHARED, codes[:, unit, :], planes[:, unit, :], hidden(unit, accs, bank, nc.scalar.copy, col_tag=f"third{third}"), ys[third])

        for third in range(THIRDS):
            tok = slice(third * C, (third + 1) * C)
            parts = []
            for r, tag in enumerate(("part", f"third{third}")):
                part = keep.tile([P, C], F32, name="part", tag=tag, align_bytes=64)
                nc.vector.tensor_tensor(part[:], y_sb[:].indirect(pos_sb[r][:, third * C // PER_COLUMN : (third + 1) * C // PER_COLUMN]), gate_sb[:, r, tok], MULT)
                parts.append(part)
            partial = ring.tile([P, C], F32, name="partial")
            nc.vector.tensor_tensor(partial[:], parts[0][:], ys[third], ADD)
            total = ring.tile([P, C], F32, name="total")
            nc.vector.tensor_tensor(total[:], partial[:], parts[1][:], ADD)
            nc.sync.dma_start(out[:, tok], total[:])
